import numpy as np
import ml_dtypes


def mxq(x, axis, fmt="e4m3"):
    dtype, down = {"e4m3": (ml_dtypes.float8_e4m3fn, 7), "e5m2": (ml_dtypes.float8_e5m2, 14)}[fmt]
    v = np.moveaxis(np.asarray(x, np.float32).astype(ml_dtypes.bfloat16).astype(np.float64), axis, -1)
    blocks = v.reshape(v.shape[:-1] + (-1, 32))
    amax = np.abs(blocks).max(-1, keepdims=True)
    byte = np.maximum(np.where(amax > 0, np.frexp(amax)[1] - 1 + 127, 0) - down, 1)
    scale = np.exp2(byte - 127.0)
    codes = (blocks / scale).astype(np.float32).astype(dtype).astype(np.float64)
    return np.moveaxis((codes * scale).reshape(v.shape), -1, axis)


WIDE = False


def mx_kscale(k):
    if not WIDE:
        return np.ones(k)
    levels = np.array([10, -10, 5, -5, 0])
    if k % 512:
        return np.exp2(np.random.permutation(np.resize(levels, k // 32))).repeat(32)
    a = np.empty((k // 512, 16))
    for p in range(k // 512):
        a[p, :8] = np.random.permutation(np.resize(levels, 8))
        for g in range(8):
            far = levels[np.abs(levels - a[p, g]) >= 10]
            a[p, g + 8] = far[np.random.randint(len(far))]
    return np.exp2(a.ravel()).repeat(32)


def f64(x):
    return np.asarray(x).astype(np.float64)


def striped(idx):
    return np.tile(idx.reshape(-1, 16).T, (8, 1)).astype(np.uint16)


def unstriped(offs):
    return offs[:16].T.reshape(-1).astype(np.int64)


def pack_weight(w):
    k, n = w.shape
    w = f64(np.asarray(w, np.float32).astype(ml_dtypes.bfloat16)).reshape(k // 32, 32, n)
    amax = np.abs(w).max(1)
    byte = np.clip(np.where(amax > 0, np.frexp(amax)[1] - 1 + 127 - 7, 1), 1, 254)
    scaled = (w * np.exp2(127.0 - byte)[:, None, :]).reshape(k, n).astype(np.float32)
    words = np.ascontiguousarray(scaled.reshape(k // 512, 128, 4, n).transpose(0, 1, 3, 2)).astype(ml_dtypes.float8_e4m3fn).view(np.uint8)
    return words, np.ascontiguousarray(byte.astype(np.uint8).reshape(k // 512, 16, n))


def unpack_weight(words, scales):
    g, p, n, _ = words.shape
    vals = np.ascontiguousarray(words).view(ml_dtypes.float8_e4m3fn).astype(np.float64) * np.repeat(np.exp2(scales.astype(np.float64) - 127.0), 8, axis=1)[..., None]
    return vals.transpose(0, 1, 3, 2).reshape(g * 512, n)


def relu(v):
    return np.maximum(v, 0.0)


K, T, D, S, V, N = 1024, 1024, 4, 2048, 512, 256


def setup_inputs():
    n = np.random.standard_normal
    s = mx_kscale(K)[:, None]
    words, scales = pack_weight(n((K, N)) / np.sqrt(K) / s)
    return {
        "xT": (n((K, T)) * s).astype(np.float32),
        "w_words": words,
        "w_scales": scales,
        "b": (0.3 * n((N, 1))).astype(np.float32),
        "gate": np.tile(np.random.uniform(0.2, 1.0, (D, 1, V)) / np.sqrt(D), (1, N, 1)).astype(np.float32),
        "pos1": striped(np.random.permutation(T)[:V]),
        "pos2": striped(np.random.permutation(T)[:V]),
        "pos3": striped(np.random.permutation(T)[:V]),
        "pos4": striped(np.random.permutation(T)[:V]),
    }


def reference(xT, w_words, w_scales, b, gate, pos1, pos2, pos3, pos4):
    w = unpack_weight(w_words, w_scales)
    y = w.T @ mxq(f64(xT), 0, "e4m3")
    y = relu(y + f64(b))
    return sum(f64(gate[d]) * y[:, unstriped(p)] for d, p in enumerate((pos1, pos2, pos3, pos4)))

@@ -1,0 +1,142 @@
+from contextlib import ExitStack
+
+import concourse.mybir as mybir
+
+K, T, D, V, N = 1024, 1024, 4, 512, 256
+FLOPS = 2 * K * N * T + 2 * D * N * V
+
+F32 = mybir.dt.float32
+BF16 = mybir.dt.bfloat16
+U32 = mybir.dt.uint32
+I32 = mybir.dt.int32
+U16 = mybir.dt.uint16
+U8 = mybir.dt.uint8
+FP8X4 = mybir.dt.float8_e4m3fn_x4
+MULT, ADD = mybir.AluOpType.mult, mybir.AluOpType.add
+RELU = mybir.ActivationFunctionType.Relu
+
+P = 128
+PACK = 4
+K_PASS = P * PACK
+PASSES = K // K_PASS
+BLOCKS = N // P
+UNIT = 256
+VECTOR_NODES = 160
+
+
+def tile_picked_agg_lin_relu_sub_l_kernel(tc, xT, w_words, w_scales, b, gate, pos1, pos2, pos3, pos4, out):
+    nc = tc.nc
+    with ExitStack() as ctx:
+        lists_pool = ctx.enter_context(tc.tile_pool(name="lists", bufs=1))
+        keep = ctx.enter_context(tc.tile_pool(name="keep", bufs=1))
+        psum = ctx.enter_context(tc.psum_pool(name="psum", bufs=1))
+
+        warm = keep.tile([P, 1], F32, name="warm")
+        nc.vector.memset(warm[:], 0.0)
+        w_sc = keep.tile([P, PASSES, N], U8, name="w_sc", align_bytes=64)
+        nc.vector.memset(w_sc[:].rearrange("p a n -> p (a n)").bitcast(I32), 0)
+        for q in range(4):
+            nc.scalar.dma_start(
+                out=w_sc[32 * q : 32 * q + 4, :, :].bitcast(I32),
+                in_=w_scales[:, 4 * q : 4 * q + 4, :].bitcast(I32).rearrange("a q n -> q a n"),
+            )
+        bias = []
+        for m in range(BLOCKS):
+            bias_m = keep.tile([P, 1], F32, name=f"bias{m}")
+            nc.scalar.dma_start(out=bias_m[:], in_=b[P * m : P * (m + 1), :])
+            bias.append(bias_m)
+        nc.scalar.activation(warm[:], warm[:], RELU)
+
+        def load_w(m):
+            w_m = keep.tile([P, PASSES, P], U32, name=f"w{m}", align_bytes=64)
+            nc.sync.dma_start(
+                out=w_m[:].bitcast(I32),
+                in_=w_words.rearrange("a p n r -> p a (n r)")[:, :, 4 * P * m : 4 * P * (m + 1)].bitcast(I32),
+            )
+            return w_m
+
+        def load_x(g, n0, n1):
+            x_c = keep.tile([P, PACK, n1 - n0], F32, name=f"x{g}_{n0}")
+            nc.sync.dma_start(out=x_c[:], in_=xT[K_PASS * g : K_PASS * (g + 1), n0:n1].rearrange("(p t) n -> p t n", t=PACK))
+            return x_c
+
+        w = {}
+        chunks = []
+        for g, n0, n1 in ((0, 0, 512), (0, 512, 1024), (1, 0, 512), (1, 512, 768), (1, 768, 1024)):
+            chunks.append((g, n0, n1, load_x(g, n0, n1)))
+            if len(chunks) == 1:
+                w[0] = load_w(0)
+        offsets = []
+        for d, pos in enumerate((pos1, pos2, pos3, pos4)):
+            offs_d = lists_pool.tile([P, V // 16], U16, name=f"offs{d}")
+            nc.sync.dma_start(offs_d[:], pos)
+            offsets.append(offs_d)
+        gates = {}
+        for m in range(BLOCKS):
+            for d in range(D):
+                gate_md = keep.tile([P, V], F32, name=f"gate{m}_{d}")
+                nc.sync.dma_start(out=gate_md[:], in_=gate[d, P * m : P * (m + 1), :])
+                gates[m, d] = gate_md
+                if (m, d) == (0, 1):
+                    w[1] = load_w(1)
+
+        codes = keep.tile([P, PASSES, T], U32, name="codes", align_bytes=64)
+        scales = keep.tile([P, PASSES, T], U8, name="scales", align_bytes=64)
+        y = [keep.tile([P, T], F32, name=f"y{m}") for m in range(BLOCKS)]
+
+        def project(acc, m, g, n0, n1):
+            nc.tensor.matmul_mx(
+                out=acc[:],
+                lhsT=w[m][:, g, :].bitcast(FP8X4),
+                lhsT_scale=w_sc[:, g, P * m : P * (m + 1)],
+                rhs=codes[:, g, n0:n1].bitcast(FP8X4),
+                rhs_scale=scales[:, g, n0:n1],
+                start=(g == 0),
+                stop=(g == PASSES - 1),
+            )
+
+        def activate(acc, m, n0, n1):
+            nc.scalar.activation(y[m][:, n0:n1], acc[:], RELU, bias=bias[m][:])
+
+        acc0 = {n0: psum.tile([P, UNIT], F32, name=f"acc0_{n0}") for n0 in range(0, T, UNIT)}
+        for g, n0, n1, x_c in chunks:
+            for u0 in range(n0, n1, UNIT):
+                grouped = keep.tile([P, UNIT, PACK], BF16, name=f"grouped{g}_{u0}", align_bytes=64)
+                src = x_c[:, :, u0 - n0 : u0 - n0 + UNIT].rearrange("p t n -> p n t")
+                nc.vector.tensor_copy(grouped[:, :VECTOR_NODES, :], src[:, :VECTOR_NODES, :])
+                nc.scalar.copy(grouped[:, VECTOR_NODES:, :], src[:, VECTOR_NODES:, :])
+                nc.vector.quantize_mx(
+                    out=codes[:, g, u0 : u0 + UNIT].bitcast(FP8X4),
+                    scales=scales[:, g, u0 : u0 + UNIT],
+                    in_=grouped[:].rearrange("p n t -> p (n t)"),
+                )
+                project(acc0[u0], 0, g, u0, u0 + UNIT)
+                if g == PASSES - 1:
+                    activate(acc0[u0], 0, u0, u0 + UNIT)
+        for n0 in range(0, T, 512):
+            acc1 = psum.tile([P, 512], F32, name=f"acc1_{n0}")
+            for g in range(PASSES):
+                project(acc1, 1, g, n0, n0 + 512)
+            activate(acc1, 1, n0, n0 + 512)
+
+        half = V // 2
+        for m in range(BLOCKS):
+            prod = [keep.tile([P, V], F32, name=f"prod{m}_{d}") for d in range(D)]
+            sums = [keep.tile([P, V], F32, name=f"sum{m}_{d}") for d in range(D - 1)]
+
+            def pick(d, v0, v1):
+                nc.vector.tensor_tensor(
+                    prod[d][:, v0:v1], y[m][:].indirect(offsets[d][:, v0 // 16 : v1 // 16]), gates[m, d][:, v0:v1], MULT
+                )
+
+            pick(0, 0, V)
+            pick(1, 0, V)
+            pick(2, 0, V)
+            nc.vector.tensor_tensor(sums[0][:], prod[0][:], prod[1][:], ADD)
+            pick(3, 0, half)
+            nc.vector.tensor_tensor(sums[1][:], sums[0][:], prod[2][:], ADD)
+            pick(3, half, V)
+            for v0 in (0, half):
+                cols = slice(v0, v0 + half)
+                nc.vector.tensor_tensor(sums[2][:, cols], sums[1][:, cols], prod[3][:, cols], ADD)
+                nc.sync.dma_start(out=out[P * m : P * (m + 1), cols], in_=sums[2][:, cols])

@@ -1,6 +1,7 @@
 from contextlib import ExitStack
 
 import concourse.mybir as mybir
+from concourse.masks import make_identity
 
 K, T, D, V, N = 1024, 1024, 4, 512, 256
 FLOPS = 2 * K * N * T + 2 * D * N * V
@@ -20,8 +21,14 @@ PACK = 4
 K_PASS = P * PACK
 PASSES = K // K_PASS
 BLOCKS = N // P
-UNIT = 256
-VECTOR_NODES = 160
+LOADS = (
+    (0, 0, 512, ((0, 512, 352),)),
+    (0, 512, 1024, ((512, 1024, 864),)),
+    (1, 0, 512, ((0, 512, 352),)),
+    (1, 512, 896, ((512, 768, 688), (768, 896, 856))),
+    (1, 896, 1024, ((896, 1024, 992),)),
+)
+GROUPS0 = ((0, 512), (512, 768), (768, 896), (896, 1024))
 
 
 def tile_picked_agg_lin_relu_sub_l_kernel(tc, xT, w_words, w_scales, b, gate, pos1, pos2, pos3, pos4, out):
@@ -35,17 +42,11 @@ def tile_picked_agg_lin_relu_sub_l_kernel(tc, xT, w_words, w_scales, b, gate, po
         nc.vector.memset(warm[:], 0.0)
         w_sc = keep.tile([P, PASSES, N], U8, name="w_sc", align_bytes=64)
         nc.vector.memset(w_sc[:].rearrange("p a n -> p (a n)").bitcast(I32), 0)
-        for q in range(4):
-            nc.scalar.dma_start(
-                out=w_sc[32 * q : 32 * q + 4, :, :].bitcast(I32),
-                in_=w_scales[:, 4 * q : 4 * q + 4, :].bitcast(I32).rearrange("a q n -> q a n"),
-            )
-        bias = []
-        for m in range(BLOCKS):
-            bias_m = keep.tile([P, 1], F32, name=f"bias{m}")
-            nc.scalar.dma_start(out=bias_m[:], in_=b[P * m : P * (m + 1), :])
-            bias.append(bias_m)
+        b_rows = keep.tile([P, P], F32, name="b_rows")
+        nc.vector.memset(b_rows[:], 0.0)
         nc.scalar.activation(warm[:], warm[:], RELU)
+        ident = keep.tile([P, P], F32, name="ident")
+        make_identity(nc, ident[:])
 
         def load_w(m):
             w_m = keep.tile([P, PASSES, P], U32, name=f"w{m}", align_bytes=64)
@@ -62,23 +63,34 @@ def tile_picked_agg_lin_relu_sub_l_kernel(tc, xT, w_words, w_scales, b, gate, po
 
         w = {}
         chunks = []
-        for g, n0, n1 in ((0, 0, 512), (0, 512, 1024), (1, 0, 512), (1, 512, 768), (1, 768, 1024)):
-            chunks.append((g, n0, n1, load_x(g, n0, n1)))
+        for g, n0, n1, units in LOADS:
+            chunks.append((g, n0, units, load_x(g, n0, n1)))
             if len(chunks) == 1:
                 w[0] = load_w(0)
+                for q in range(4):
+                    nc.sync.dma_start(
+                        out=w_sc[32 * q : 32 * q + 4, :, :].bitcast(I32),
+                        in_=w_scales[:, 4 * q : 4 * q + 4, :].bitcast(I32).rearrange("a q n -> q a n"),
+                    )
+                nc.sync.dma_start(out=b_rows[:BLOCKS, :], in_=b.rearrange("(m p) o -> m (p o)", p=P))
         offsets = []
-        for d, pos in enumerate((pos1, pos2, pos3, pos4)):
-            offs_d = lists_pool.tile([P, V // 16], U16, name=f"offs{d}")
-            nc.sync.dma_start(offs_d[:], pos)
-            offsets.append(offs_d)
         gates = {}
         for m in range(BLOCKS):
-            for d in range(D):
+            for d, pos in enumerate((pos1, pos2, pos3, pos4)):
+                if m == 0:
+                    offs_d = lists_pool.tile([P, V // 16], U16, name=f"offs{d}")
+                    nc.sync.dma_start(offs_d[:], pos)
+                    offsets.append(offs_d)
                 gate_md = keep.tile([P, V], F32, name=f"gate{m}_{d}")
                 nc.sync.dma_start(out=gate_md[:], in_=gate[d, P * m : P * (m + 1), :])
                 gates[m, d] = gate_md
-                if (m, d) == (0, 1):
+                if (m, d) == (0, 2):
                     w[1] = load_w(1)
+
+        b_turned = psum.tile([P, P], F32, name="b_turned")
+        nc.tensor.transpose(b_turned[:], b_rows[:], ident[:])
+        bias = keep.tile([P, BLOCKS], F32, name="bias")
+        nc.scalar.copy(bias[:], b_turned[:, :BLOCKS])
 
         codes = keep.tile([P, PASSES, T], U32, name="codes", align_bytes=64)
         scales = keep.tile([P, PASSES, T], U8, name="scales", align_bytes=64)
@@ -96,47 +108,53 @@ def tile_picked_agg_lin_relu_sub_l_kernel(tc, xT, w_words, w_scales, b, gate, po
             )
 
         def activate(acc, m, n0, n1):
-            nc.scalar.activation(y[m][:, n0:n1], acc[:], RELU, bias=bias[m][:])
+            nc.scalar.activation(y[m][:, n0:n1], acc[:], RELU, bias=bias[:, m : m + 1])
 
-        acc0 = {n0: psum.tile([P, UNIT], F32, name=f"acc0_{n0}") for n0 in range(0, T, UNIT)}
-        for g, n0, n1, x_c in chunks:
-            for u0 in range(n0, n1, UNIT):
-                grouped = keep.tile([P, UNIT, PACK], BF16, name=f"grouped{g}_{u0}", align_bytes=64)
-                src = x_c[:, :, u0 - n0 : u0 - n0 + UNIT].rearrange("p t n -> p n t")
-                nc.vector.tensor_copy(grouped[:, :VECTOR_NODES, :], src[:, :VECTOR_NODES, :])
-                nc.scalar.copy(grouped[:, VECTOR_NODES:, :], src[:, VECTOR_NODES:, :])
+        acc0 = {n0: psum.tile([P, n1 - n0], F32, name=f"acc0_{n0}") for n0, n1 in GROUPS0}
+        for g, load0, units, x_c in chunks:
+            for u0, u1, share in units:
+                grouped = keep.tile([P, u1 - u0, PACK], BF16, name=f"grouped{g}_{u0}", align_bytes=64)
+                src = x_c[:].rearrange("p t n -> p n t")
+                nc.vector.tensor_copy(grouped[:, : share - u0, :], src[:, u0 - load0 : share - load0, :])
+                nc.scalar.copy(grouped[:, share - u0 :, :], src[:, share - load0 : u1 - load0, :])
                 nc.vector.quantize_mx(
-                    out=codes[:, g, u0 : u0 + UNIT].bitcast(FP8X4),
-                    scales=scales[:, g, u0 : u0 + UNIT],
+                    out=codes[:, g, u0:u1].bitcast(FP8X4),
+                    scales=scales[:, g, u0:u1],
                     in_=grouped[:].rearrange("p n t -> p (n t)"),
                 )
-                project(acc0[u0], 0, g, u0, u0 + UNIT)
-                if g == PASSES - 1:
-                    activate(acc0[u0], 0, u0, u0 + UNIT)
+                for n0, n1 in GROUPS0:
+                    if u0 <= n0 and n1 <= u1:
+                        project(acc0[n0], 0, g, n0, n1)
+                        if g == PASSES - 1:
+                            activate(acc0[n0], 0, n0, n1)
         for n0 in range(0, T, 512):
             acc1 = psum.tile([P, 512], F32, name=f"acc1_{n0}")
             for g in range(PASSES):
                 project(acc1, 1, g, n0, n0 + 512)
             activate(acc1, 1, n0, n0 + 512)
 
-        half = V // 2
-        for m in range(BLOCKS):
-            prod = [keep.tile([P, V], F32, name=f"prod{m}_{d}") for d in range(D)]
-            sums = [keep.tile([P, V], F32, name=f"sum{m}_{d}") for d in range(D - 1)]
+        prods = [keep.tile([P, D, V], F32, name=f"prod{m}") for m in range(BLOCKS)]
 
-            def pick(d, v0, v1):
-                nc.vector.tensor_tensor(
-                    prod[d][:, v0:v1], y[m][:].indirect(offsets[d][:, v0 // 16 : v1 // 16]), gates[m, d][:, v0:v1], MULT
-                )
+        def pick(m, d):
+            nc.vector.tensor_tensor(prods[m][:, d, :], y[m][:].indirect(offsets[d][:]), gates[m, d][:], MULT)
 
-            pick(0, 0, V)
-            pick(1, 0, V)
-            pick(2, 0, V)
-            nc.vector.tensor_tensor(sums[0][:], prod[0][:], prod[1][:], ADD)
-            pick(3, 0, half)
-            nc.vector.tensor_tensor(sums[1][:], sums[0][:], prod[2][:], ADD)
-            pick(3, half, V)
-            for v0 in (0, half):
-                cols = slice(v0, v0 + half)
-                nc.vector.tensor_tensor(sums[2][:, cols], sums[1][:, cols], prod[3][:, cols], ADD)
-                nc.sync.dma_start(out=out[P * m : P * (m + 1), cols], in_=sums[2][:, cols])
+        for d in range(D):
+            pick(0, d)
+        pick(1, 0)
+        pair0 = keep.tile([P, 2, V], F32, name="pair0")
+        nc.vector.tensor_tensor(pair0[:], prods[0][:, 0:2, :], prods[0][:, 2:4, :], ADD)
+        pick(1, 1)
+        sum0 = keep.tile([P, V], F32, name="sum0")
+        nc.vector.tensor_tensor(sum0[:], pair0[:, 0, :], pair0[:, 1, :], ADD)
+        nc.sync.dma_start(out=out[:P, :], in_=sum0[:])
+        pick(1, 2)
+        two1 = keep.tile([P, V], F32, name="two1")
+        nc.vector.tensor_tensor(two1[:], prods[1][:, 0, :], prods[1][:, 1, :], ADD)
+        pick(1, 3)
+        three1 = keep.tile([P, V], F32, name="three1")
+        nc.vector.tensor_tensor(three1[:], two1[:], prods[1][:, 2, :], ADD)
+        sum1 = keep.tile([P, V], F32, name="sum1")
+        for v0 in range(0, V, V // 2):
+            cols = slice(v0, v0 + V // 2)
+            nc.vector.tensor_tensor(sum1[:, cols], three1[:, cols], prods[1][:, 3, cols], ADD)
+            nc.sync.dma_start(out=out[P:, cols], in_=sum1[:, cols])

@@ -21,12 +21,12 @@ PACK = 4
 K_PASS = P * PACK
 PASSES = K // K_PASS
 BLOCKS = N // P
-LOADS = (
-    (0, 0, 512, ((0, 512, 352),)),
-    (0, 512, 1024, ((512, 1024, 864),)),
-    (1, 0, 512, ((0, 512, 352),)),
-    (1, 512, 896, ((512, 768, 688), (768, 896, 856))),
-    (1, 896, 1024, ((896, 1024, 992),)),
+HALF = 512
+HALF_SHARE = 320
+LOADS1 = (
+    (0, 512, ((0, 512, 352),)),
+    (512, 896, ((512, 768, 688), (768, 896, 856))),
+    (896, 1024, ((896, 1024, 992),)),
 )
 GROUPS0 = ((0, 512), (512, 768), (768, 896), (896, 1024))
 
@@ -56,16 +56,13 @@ def tile_picked_agg_lin_relu_sub_l_kernel(tc, xT, w_words, w_scales, b, gate, po
             )
             return w_m
 
-        def load_x(g, n0, n1):
-            x_c = keep.tile([P, PACK, n1 - n0], F32, name=f"x{g}_{n0}")
-            nc.sync.dma_start(out=x_c[:], in_=xT[K_PASS * g : K_PASS * (g + 1), n0:n1].rearrange("(p t) n -> p t n", t=PACK))
-            return x_c
-
         w = {}
-        chunks = []
-        for g, n0, n1, units in LOADS:
-            chunks.append((g, n0, units, load_x(g, n0, n1)))
-            if len(chunks) == 1:
+        pairs = []
+        for h in range(2):
+            x_h = keep.tile([P, 2, T], F32, name=f"x0_{h}")
+            nc.sync.dma_start(out=x_h[:], in_=xT[:K_PASS, :].rearrange("(p t) n -> p t n", t=PACK)[:, 2 * h : 2 * h + 2, :])
+            pairs.append(x_h)
+            if h == 0:
                 w[0] = load_w(0)
                 for q in range(4):
                     nc.sync.dma_start(
@@ -73,6 +70,11 @@ def tile_picked_agg_lin_relu_sub_l_kernel(tc, xT, w_words, w_scales, b, gate, po
                         in_=w_scales[:, 4 * q : 4 * q + 4, :].bitcast(I32).rearrange("a q n -> q a n"),
                     )
                 nc.sync.dma_start(out=b_rows[:BLOCKS, :], in_=b.rearrange("(m p) o -> m (p o)", p=P))
+        chunks = []
+        for n0, n1, units in LOADS1:
+            x_c = keep.tile([P, PACK, n1 - n0], F32, name=f"x1_{n0}")
+            nc.sync.dma_start(out=x_c[:], in_=xT[K_PASS:, n0:n1].rearrange("(p t) n -> p t n", t=PACK))
+            chunks.append((n0, units, x_c))
         offsets = []
         gates = {}
         for m in range(BLOCKS):
@@ -111,22 +113,36 @@ def tile_picked_agg_lin_relu_sub_l_kernel(tc, xT, w_words, w_scales, b, gate, po
             nc.scalar.activation(y[m][:, n0:n1], acc[:], RELU, bias=bias[:, m : m + 1])
 
         acc0 = {n0: psum.tile([P, n1 - n0], F32, name=f"acc0_{n0}") for n0, n1 in GROUPS0}
-        for g, load0, units, x_c in chunks:
+
+        def quantise(g, u0, u1, grouped):
+            nc.vector.quantize_mx(
+                out=codes[:, g, u0:u1].bitcast(FP8X4),
+                scales=scales[:, g, u0:u1],
+                in_=grouped.rearrange("p n t -> p (n t)"),
+            )
+            for n0, n1 in GROUPS0:
+                if u0 <= n0 and n1 <= u1:
+                    project(acc0[n0], 0, g, n0, n1)
+                    if g == PASSES - 1:
+                        activate(acc0[n0], 0, n0, n1)
+
+        grouped0 = [keep.tile([P, HALF, PACK], BF16, name=f"grouped0_{u}", align_bytes=64) for u in range(2)]
+        for h in range(2):
+            src = pairs[h][:].rearrange("p t n -> p n t")
+            for u in range(2):
+                dst = grouped0[u][:, :, 2 * h : 2 * h + 2]
+                u0 = HALF * u
+                nc.vector.tensor_copy(dst[:, :HALF_SHARE, :], src[:, u0 : u0 + HALF_SHARE, :])
+                nc.scalar.copy(dst[:, HALF_SHARE:, :], src[:, u0 + HALF_SHARE : u0 + HALF, :])
+        for u in range(2):
+            quantise(0, HALF * u, HALF * (u + 1), grouped0[u][:])
+        for load0, units, x_c in chunks:
+            src = x_c[:].rearrange("p t n -> p n t")
             for u0, u1, share in units:
-                grouped = keep.tile([P, u1 - u0, PACK], BF16, name=f"grouped{g}_{u0}", align_bytes=64)
-                src = x_c[:].rearrange("p t n -> p n t")
+                grouped = keep.tile([P, u1 - u0, PACK], BF16, name=f"grouped1_{u0}", align_bytes=64)
                 nc.vector.tensor_copy(grouped[:, : share - u0, :], src[:, u0 - load0 : share - load0, :])
                 nc.scalar.copy(grouped[:, share - u0 :, :], src[:, share - load0 : u1 - load0, :])
-                nc.vector.quantize_mx(
-                    out=codes[:, g, u0:u1].bitcast(FP8X4),
-                    scales=scales[:, g, u0:u1],
-                    in_=grouped[:].rearrange("p n t -> p (n t)"),
-                )
-                for n0, n1 in GROUPS0:
-                    if u0 <= n0 and n1 <= u1:
-                        project(acc0[n0], 0, g, n0, n1)
-                        if g == PASSES - 1:
-                            activate(acc0[n0], 0, n0, n1)
+                quantise(1, u0, u1, grouped[:])
         for n0 in range(0, T, 512):
             acc1 = psum.tile([P, 512], F32, name=f"acc1_{n0}")
             for g in range(PASSES):
@@ -134,9 +150,12 @@ def tile_picked_agg_lin_relu_sub_l_kernel(tc, xT, w_words, w_scales, b, gate, po
             activate(acc1, 1, n0, n0 + 512)
 
         prods = [keep.tile([P, D, V], F32, name=f"prod{m}") for m in range(BLOCKS)]
+        halves = ((0, V // 2), (V // 2, V))
 
-        def pick(m, d):
-            nc.vector.tensor_tensor(prods[m][:, d, :], y[m][:].indirect(offsets[d][:]), gates[m, d][:], MULT)
+        def pick(m, d, v0=0, v1=V):
+            nc.vector.tensor_tensor(
+                prods[m][:, d, v0:v1], y[m][:].indirect(offsets[d][:, v0 // 16 : v1 // 16]), gates[m, d][:, v0:v1], MULT
+            )
 
         for d in range(D):
             pick(0, d)
@@ -150,11 +169,11 @@ def tile_picked_agg_lin_relu_sub_l_kernel(tc, xT, w_words, w_scales, b, gate, po
         pick(1, 2)
         two1 = keep.tile([P, V], F32, name="two1")
         nc.vector.tensor_tensor(two1[:], prods[1][:, 0, :], prods[1][:, 1, :], ADD)
-        pick(1, 3)
+        pick(1, 3, *halves[0])
         three1 = keep.tile([P, V], F32, name="three1")
         nc.vector.tensor_tensor(three1[:], two1[:], prods[1][:, 2, :], ADD)
+        pick(1, 3, *halves[1])
         sum1 = keep.tile([P, V], F32, name="sum1")
-        for v0 in range(0, V, V // 2):
-            cols = slice(v0, v0 + V // 2)
-            nc.vector.tensor_tensor(sum1[:, cols], three1[:, cols], prods[1][:, 3, cols], ADD)
-            nc.sync.dma_start(out=out[P:, cols], in_=sum1[:, cols])
+        for v0, v1 in halves:
+            nc.vector.tensor_tensor(sum1[:, v0:v1], three1[:, v0:v1], prods[1][:, 3, v0:v1], ADD)
+            nc.sync.dma_start(out=out[P:, v0:v1], in_=sum1[:, v0:v1])

@@ -24,9 +24,10 @@ BLOCKS = N // P
 HALF = 512
 HALF_SHARE = 320
 LOADS1 = (
-    (0, 512, ((0, 512, 352),)),
-    (512, 896, ((512, 768, 688), (768, 896, 856))),
-    (896, 1024, ((896, 1024, 992),)),
+    (0, 512, ((0, 512, 336),)),
+    (512, 768, ((512, 768, 672),)),
+    (768, 896, ((768, 896, 848),)),
+    (896, 1024, ((896, 1024, 1000),)),
 )
 GROUPS0 = ((0, 512), (512, 768), (768, 896), (896, 1024))
 
@@ -44,6 +45,12 @@ def tile_picked_agg_lin_relu_sub_l_kernel(tc, xT, w_words, w_scales, b, gate, po
         nc.vector.memset(w_sc[:].rearrange("p a n -> p (a n)").bitcast(I32), 0)
         b_rows = keep.tile([P, P], F32, name="b_rows")
         nc.vector.memset(b_rows[:], 0.0)
+        for q in range(4):
+            nc.scalar.dma_start(
+                out=w_sc[32 * q : 32 * q + 4, :, :].bitcast(I32),
+                in_=w_scales[:, 4 * q : 4 * q + 4, :].bitcast(I32).rearrange("a q n -> q a n"),
+            )
+        nc.scalar.dma_start(out=b_rows[:BLOCKS, :], in_=b.rearrange("(m p) o -> m (p o)", p=P))
         nc.scalar.activation(warm[:], warm[:], RELU)
         ident = keep.tile([P, P], F32, name="ident")
         make_identity(nc, ident[:])
@@ -64,12 +71,6 @@ def tile_picked_agg_lin_relu_sub_l_kernel(tc, xT, w_words, w_scales, b, gate, po
             pairs.append(x_h)
             if h == 0:
                 w[0] = load_w(0)
-                for q in range(4):
-                    nc.sync.dma_start(
-                        out=w_sc[32 * q : 32 * q + 4, :, :].bitcast(I32),
-                        in_=w_scales[:, 4 * q : 4 * q + 4, :].bitcast(I32).rearrange("a q n -> q a n"),
-                    )
-                nc.sync.dma_start(out=b_rows[:BLOCKS, :], in_=b.rearrange("(m p) o -> m (p o)", p=P))
         chunks = []
         for n0, n1, units in LOADS1:
             x_c = keep.tile([P, PACK, n1 - n0], F32, name=f"x1_{n0}")
@@ -126,22 +127,24 @@ def tile_picked_agg_lin_relu_sub_l_kernel(tc, xT, w_words, w_scales, b, gate, po
                     if g == PASSES - 1:
                         activate(acc0[n0], 0, n0, n1)
 
+        def interleave(dst, src, share):
+            nodes = dst.shape[1]
+            for copy, n0, n1 in ((nc.vector.tensor_copy, 0, share), (nc.scalar.copy, share, nodes)):
+                copy(
+                    dst[:, n0:n1, :].rearrange("p (c i) t -> p c t i", i=4),
+                    src[:, :, n0:n1].rearrange("p t (c i) -> p c t i", i=4),
+                )
+
         grouped0 = [keep.tile([P, HALF, PACK], BF16, name=f"grouped0_{u}", align_bytes=64) for u in range(2)]
         for h in range(2):
-            src = pairs[h][:].rearrange("p t n -> p n t")
             for u in range(2):
-                dst = grouped0[u][:, :, 2 * h : 2 * h + 2]
-                u0 = HALF * u
-                nc.vector.tensor_copy(dst[:, :HALF_SHARE, :], src[:, u0 : u0 + HALF_SHARE, :])
-                nc.scalar.copy(dst[:, HALF_SHARE:, :], src[:, u0 + HALF_SHARE : u0 + HALF, :])
+                interleave(grouped0[u][:, :, 2 * h : 2 * h + 2], pairs[h][:, :, HALF * u : HALF * (u + 1)], HALF_SHARE)
         for u in range(2):
             quantise(0, HALF * u, HALF * (u + 1), grouped0[u][:])
         for load0, units, x_c in chunks:
-            src = x_c[:].rearrange("p t n -> p n t")
             for u0, u1, share in units:
                 grouped = keep.tile([P, u1 - u0, PACK], BF16, name=f"grouped1_{u0}", align_bytes=64)
-                nc.vector.tensor_copy(grouped[:, : share - u0, :], src[:, u0 - load0 : share - load0, :])
-                nc.scalar.copy(grouped[:, share - u0 :, :], src[:, share - load0 : u1 - load0, :])
+                interleave(grouped[:], x_c[:, :, u0 - load0 : u1 - load0], share - u0)
                 quantise(1, u0, u1, grouped[:])
         for n0 in range(0, T, 512):
             acc1 = psum.tile([P, 512], F32, name=f"acc1_{n0}")

from contextlib import ExitStack

import concourse.mybir as mybir
from concourse.masks import make_identity

K, T, D, V, N = 1024, 1024, 4, 512, 256
FLOPS = 2 * K * N * T + 2 * D * N * V

F32 = mybir.dt.float32
BF16 = mybir.dt.bfloat16
U32 = mybir.dt.uint32
I32 = mybir.dt.int32
U16 = mybir.dt.uint16
U8 = mybir.dt.uint8
FP8X4 = mybir.dt.float8_e4m3fn_x4
MULT, ADD = mybir.AluOpType.mult, mybir.AluOpType.add
RELU = mybir.ActivationFunctionType.Relu

P = 128
PACK = 4
K_PASS = P * PACK
PASSES = K // K_PASS
BLOCKS = N // P
HALF = 512
HALF_SHARE = 320
LOADS1 = (
    (0, 512, ((0, 512, 336),)),
    (512, 768, ((512, 768, 672),)),
    (768, 896, ((768, 896, 848),)),
    (896, 1024, ((896, 1024, 1000),)),
)
GROUPS0 = ((0, 512), (512, 768), (768, 896), (896, 1024))


def tile_picked_agg_lin_relu_sub_l_kernel(tc, xT, w_words, w_scales, b, gate, pos1, pos2, pos3, pos4, out):
    nc = tc.nc
    with ExitStack() as ctx:
        lists_pool = ctx.enter_context(tc.tile_pool(name="lists", bufs=1))
        keep = ctx.enter_context(tc.tile_pool(name="keep", bufs=1))
        psum = ctx.enter_context(tc.psum_pool(name="psum", bufs=1))

        warm = keep.tile([P, 1], F32, name="warm")
        nc.vector.memset(warm[:], 0.0)
        w_sc = keep.tile([P, PASSES, N], U8, name="w_sc", align_bytes=64)
        nc.vector.memset(w_sc[:].rearrange("p a n -> p (a n)").bitcast(I32), 0)
        b_rows = keep.tile([P, P], F32, name="b_rows")
        nc.vector.memset(b_rows[:], 0.0)
        for q in range(4):
            nc.scalar.dma_start(
                out=w_sc[32 * q : 32 * q + 4, :, :].bitcast(I32),
                in_=w_scales[:, 4 * q : 4 * q + 4, :].bitcast(I32).rearrange("a q n -> q a n"),
            )
        nc.scalar.dma_start(out=b_rows[:BLOCKS, :], in_=b.rearrange("(m p) o -> m (p o)", p=P))
        nc.scalar.activation(warm[:], warm[:], RELU)
        ident = keep.tile([P, P], F32, name="ident")
        make_identity(nc, ident[:])

        def load_w(m):
            w_m = keep.tile([P, PASSES, P], U32, name=f"w{m}", align_bytes=64)
            nc.sync.dma_start(
                out=w_m[:].bitcast(I32),
                in_=w_words.rearrange("a p n r -> p a (n r)")[:, :, 4 * P * m : 4 * P * (m + 1)].bitcast(I32),
            )
            return w_m

        w = {}
        pairs = []
        for h in range(2):
            x_h = keep.tile([P, 2, T], F32, name=f"x0_{h}")
            nc.sync.dma_start(out=x_h[:], in_=xT[:K_PASS, :].rearrange("(p t) n -> p t n", t=PACK)[:, 2 * h : 2 * h + 2, :])
            pairs.append(x_h)
            if h == 0:
                w[0] = load_w(0)
        chunks = []
        for n0, n1, units in LOADS1:
            x_c = keep.tile([P, PACK, n1 - n0], F32, name=f"x1_{n0}")
            nc.sync.dma_start(out=x_c[:], in_=xT[K_PASS:, n0:n1].rearrange("(p t) n -> p t n", t=PACK))
            chunks.append((n0, units, x_c))
        offsets = []
        gates = {}
        for m in range(BLOCKS):
            for d, pos in enumerate((pos1, pos2, pos3, pos4)):
                if m == 0:
                    offs_d = lists_pool.tile([P, V // 16], U16, name=f"offs{d}")
                    nc.sync.dma_start(offs_d[:], pos)
                    offsets.append(offs_d)
                gate_md = keep.tile([P, V], F32, name=f"gate{m}_{d}")
                nc.sync.dma_start(out=gate_md[:], in_=gate[d, P * m : P * (m + 1), :])
                gates[m, d] = gate_md
                if (m, d) == (0, 2):
                    w[1] = load_w(1)

        b_turned = psum.tile([P, P], F32, name="b_turned")
        nc.tensor.transpose(b_turned[:], b_rows[:], ident[:])
        bias = keep.tile([P, BLOCKS], F32, name="bias")
        nc.scalar.copy(bias[:], b_turned[:, :BLOCKS])

        codes = keep.tile([P, PASSES, T], U32, name="codes", align_bytes=64)
        scales = keep.tile([P, PASSES, T], U8, name="scales", align_bytes=64)
        y = [keep.tile([P, T], F32, name=f"y{m}") for m in range(BLOCKS)]

        def project(acc, m, g, n0, n1):
            nc.tensor.matmul_mx(
                out=acc[:],
                lhsT=w[m][:, g, :].bitcast(FP8X4),
                lhsT_scale=w_sc[:, g, P * m : P * (m + 1)],
                rhs=codes[:, g, n0:n1].bitcast(FP8X4),
                rhs_scale=scales[:, g, n0:n1],
                start=(g == 0),
                stop=(g == PASSES - 1),
            )

        def activate(acc, m, n0, n1):
            nc.scalar.activation(y[m][:, n0:n1], acc[:], RELU, bias=bias[:, m : m + 1])

        acc0 = {n0: psum.tile([P, n1 - n0], F32, name=f"acc0_{n0}") for n0, n1 in GROUPS0}

        def quantise(g, u0, u1, grouped):
            nc.vector.quantize_mx(
                out=codes[:, g, u0:u1].bitcast(FP8X4),
                scales=scales[:, g, u0:u1],
                in_=grouped.rearrange("p n t -> p (n t)"),
            )
            for n0, n1 in GROUPS0:
                if u0 <= n0 and n1 <= u1:
                    project(acc0[n0], 0, g, n0, n1)
                    if g == PASSES - 1:
                        activate(acc0[n0], 0, n0, n1)

        def interleave(dst, src, share):
            nodes = dst.shape[1]
            for copy, n0, n1 in ((nc.vector.tensor_copy, 0, share), (nc.scalar.copy, share, nodes)):
                copy(
                    dst[:, n0:n1, :].rearrange("p (c i) t -> p c t i", i=4),
                    src[:, :, n0:n1].rearrange("p t (c i) -> p c t i", i=4),
                )

        grouped0 = [keep.tile([P, HALF, PACK], BF16, name=f"grouped0_{u}", align_bytes=64) for u in range(2)]
        for h in range(2):
            for u in range(2):
                interleave(grouped0[u][:, :, 2 * h : 2 * h + 2], pairs[h][:, :, HALF * u : HALF * (u + 1)], HALF_SHARE)
        for u in range(2):
            quantise(0, HALF * u, HALF * (u + 1), grouped0[u][:])
        for load0, units, x_c in chunks:
            for u0, u1, share in units:
                grouped = keep.tile([P, u1 - u0, PACK], BF16, name=f"grouped1_{u0}", align_bytes=64)
                interleave(grouped[:], x_c[:, :, u0 - load0 : u1 - load0], share - u0)
                quantise(1, u0, u1, grouped[:])
        for n0 in range(0, T, 512):
            acc1 = psum.tile([P, 512], F32, name=f"acc1_{n0}")
            for g in range(PASSES):
                project(acc1, 1, g, n0, n0 + 512)
            activate(acc1, 1, n0, n0 + 512)

        prods = [keep.tile([P, D, V], F32, name=f"prod{m}") for m in range(BLOCKS)]
        halves = ((0, V // 2), (V // 2, V))

        def pick(m, d, v0=0, v1=V):
            nc.vector.tensor_tensor(
                prods[m][:, d, v0:v1], y[m][:].indirect(offsets[d][:, v0 // 16 : v1 // 16]), gates[m, d][:, v0:v1], MULT
            )

        for d in range(D):
            pick(0, d)
        pick(1, 0)
        pair0 = keep.tile([P, 2, V], F32, name="pair0")
        nc.vector.tensor_tensor(pair0[:], prods[0][:, 0:2, :], prods[0][:, 2:4, :], ADD)
        pick(1, 1)
        sum0 = keep.tile([P, V], F32, name="sum0")
        nc.vector.tensor_tensor(sum0[:], pair0[:, 0, :], pair0[:, 1, :], ADD)
        nc.sync.dma_start(out=out[:P, :], in_=sum0[:])
        pick(1, 2)
        two1 = keep.tile([P, V], F32, name="two1")
        nc.vector.tensor_tensor(two1[:], prods[1][:, 0, :], prods[1][:, 1, :], ADD)
        pick(1, 3, *halves[0])
        three1 = keep.tile([P, V], F32, name="three1")
        nc.vector.tensor_tensor(three1[:], two1[:], prods[1][:, 2, :], ADD)
        pick(1, 3, *halves[1])
        sum1 = keep.tile([P, V], F32, name="sum1")
        for v0, v1 in halves:
            nc.vector.tensor_tensor(sum1[:, v0:v1], three1[:, v0:v1], prods[1][:, 3, v0:v1], ADD)
            nc.sync.dma_start(out=out[P:, v0:v1], in_=sum1[:, v0:v1])
